import numpy as np, ml_dtypes
CORES = [6,15,38,47]
N = 4
BF = ml_dtypes.bfloat16
S, F, L, RO, A, TH, BYG = 4096, 1024, 256, 4, 960, 9, 0
def whole(x, hi):
    return np.minimum(x.astype(np.int64), hi)
def parts(rng):
    a = rng.choice(np.array([0.2, 0.3, 0.4, 0.5]), (N, 8, 1, 1)).astype(np.float32)
    t = whole(256 * rng.random((N, 8, 16, S), dtype=np.float32) ** a, 255)
    t = np.where(rng.random((N, 8, 1, S)) < 0.25, 255, t)
    return t, rng.integers(0, 255, (N, 8, 16, F)), rng.integers(0, S, (N, 8, 16, F)), rng.integers(0, S, (N, 8, 16, F))
def pack(t, z, eh, ef):
    return {"tab": t.reshape(N, 128, S).astype(np.float32).astype(BF), "zf": z.reshape(N, 128, F).astype(np.float32).astype(BF),
            "eh": np.ascontiguousarray(eh.reshape(N, 128, F)).astype(np.int32), "ef": np.ascontiguousarray(ef.reshape(N, 128, F)).astype(np.int32)}
def setup_inputs(rng):
    return pack(*parts(rng))
def setup_inputs_full(rng):
    t, z, eh, ef = parts(rng)
    for g in (0, 5):
        t[:, g] = 255; eh[:, g] = rng.integers(F, S, (N, 16, F)); ef[:, g] = rng.integers(F, S, (N, 16, F))
        eh[:, g, 0] = np.argsort(rng.random((N, F)), axis=1)
    f = np.arange(F); c = F - A; see = (f >= A - c) & (f < A)
    m = np.flatnonzero(see)
    for g in (2, 7):
        p = np.argsort(rng.random((N, S // 2)), axis=1)[:, :L]
        t[:, g] = 255; eh[:, g] = rng.integers(S // 2, S - 64, (N, 16, F)); ef[:, g] = rng.integers(S // 2, S - 64, (N, 16, F))
        z[:, g] = np.where(f < L, rng.integers(160, 255, (N, 16, F)), np.where(see, rng.integers(100, 160, (N, 16, F)), rng.integers(0, 100, (N, 16, F))))
        eh[:, g, 0] = np.where(see, eh[:, g, 0], p[:, f % L])
        for r in range(N):
            q = (r + 1 + (2 + BYG * g) % (N - 1)) % N
            a, b = m[1::4], m[3::4]
            ef[r, g, rng.integers(0, 16, len(a)), a] = p[q, L - c - 1]
            ef[r, g, rng.integers(0, 16, len(b)), b] = np.max(p[q])
    return pack(t, z, eh, ef)
def setup_inputs_ties(rng):
    t, z, eh, ef = parts(rng)
    pat = np.array([0, 0, 2, 3, 5, TH - 2, TH - 2, TH - 2, TH - 1, TH - 1, TH - 1, TH - 1, TH, TH, TH, 16])
    place = np.argsort(rng.random((N, 4, 16, S), dtype=np.float32), axis=2)
    t[:, :4] = np.where(place < pat[np.arange(S) % 16], 0, 255)
    for x in (eh, ef):
        top = rng.choice(np.array([8, 12, 12, 12, 15, 16]), (N, 4, 1, F))
        x[:, :4] = 16 * rng.integers(0, S // 16, (N, 4, 16, F)) + (rng.random((N, 4, 16, F)) * top).astype(np.int64)
    v = np.array([0, 1, 127, 128, 254, 255])
    t[:, 4:] = rng.choice(v, (N, 4, 16, S), p=[0.04, 0.04, 0.1, 0.12, 0.3, 0.4]); z[:, 4:] = rng.choice(v[:5], (N, 4, 16, F))
    return pack(t, z, eh, ef)
def setup_inputs_alike(rng):
    t, z, eh, ef = parts(rng); few = np.array([0, S - 1, S // 2, 3])
    eh[:, 0] = rng.choice(few, (N, 16, F)); eh[:, 1] = rng.integers(0, S, (N, 1, F))
    t[:, 2] = 255; eh[:, 2] = rng.integers(0, S, (N, 1, 1))
    eh[:, 3] = S - 1 - rng.integers(0, 12, (N, 16, F)); ef[:, 3] = S - 1 - rng.integers(0, 12, (N, 16, F))
    ef[:, 4] = rng.choice(few, (N, 16, F))
    for x in (z, eh, ef): x[:, 5, :, 1::2] = x[:, 5, :, 0::2]
    return pack(t, z, eh, ef)
def setup_inputs_hard(rng):
    t, z, eh, ef = parts(rng)
    t[:, 0] = 0; t[rng.integers(0, N), 1] = 0; t[:, 2] = 255
    z[:, 3] = 0; t[:, 3] = np.maximum(t[:, 3], 1)
    z[:, 4] = 254; t[:, 4] = np.where(rng.random((N, 16, S)) < 0.8, 255, t[:, 4])
    return pack(t, z, eh, ef)
def setup_inputs_spread(rng):
    u = np.float32(2) ** -rng.integers(-2, 6, (N, 8, 1, S)).astype(np.float32); v = np.float32(2) ** rng.integers(-2, 5, (N, 8, 1, F)).astype(np.float32)
    t = whole(256 * rng.random((N, 8, 16, S), dtype=np.float32) ** u, 255); z = whole(255 * rng.random((N, 8, 16, F), dtype=np.float32) ** v, 254)
    e = [whole(S * rng.random((N, 8, 16, F)) ** (2.0 ** rng.integers(0, 3, (N, 8, 16, 1))), S - 1) for i in range(2)]
    return pack(t, z, e[0], e[1])
def check_inputs(d):
    bad = []
    for k, hi in (("tab", 255), ("zf", 254), ("eh", S - 1), ("ef", S - 1)):
        v = np.asarray(d[k]).astype(np.float64)
        if not (np.min(v) >= 0 and np.max(v) <= hi): bad.append("range of " + k)
        if not np.all(v == np.floor(v)): bad.append("whole numbers in " + k)
    return bad
def reference(tab, zf, eh, ef):
    t = tab.astype(np.float32).astype(np.int32).reshape(N, 8, 16, S); z = zf.astype(np.float32).astype(np.int32).reshape(N, 8, 16, F)
    home = eh.astype(np.int64).reshape(N, 8, 16, F); far = ef.astype(np.int64).reshape(N, 8, 16, F)
    d = np.zeros((N, 8, F), np.int64); oc = np.full((N, 8, S), -1, np.int64); free = np.ones((N, 8, F), bool)
    for step in range(RO):
        old = np.array(t)
        turn = (np.arange(F) + A * step) % F
        for r in range(N):
            for g in range(8):
                q = (r + 1 + (step + BYG * g) % (N - 1)) % N
                ln = turn[free[r, g][turn]][:L]
                zl = z[r, g][:, ln]
                sh = (home[r, g][:, ln] + d[r, g, ln]) & (S - 1); sf = (far[r, g][:, ln] + d[r, g, ln]) & (S - 1)
                ph = np.sum(old[r, g][:, sh] <= zl[:, None, :], axis=0); pf = np.sum(old[q, g][:, sf] <= zl[:, None, :], axis=0)
                k = np.argmax(ph, axis=0)
                worst = np.maximum(np.max(ph, axis=0), np.max(pf, axis=0)); go = worst < TH
                d[r, g, ln] += np.where(go, 0, worst)
                cl = np.flatnonzero(go)
                s, first = np.unique(sh[k, np.arange(L)][cl], return_index=True)
                w = cl[first]; was = oc[r, g, s]; was = was[was >= 0]
                d[r, g, was] += 1; free[r, g, was] = True
                t[r, g][:, s] = zl[:, w]; oc[r, g, s] = ln[w]; free[r, g, ln[w]] = False
    return {"yt": t.reshape(N, 128, S).astype(np.float32).astype(BF), "yo": oc.astype(np.float32), "yd": d.astype(np.float32)}

from concourse.mybir import AluOpType, ActivationFunctionType

OP = AluOpType
AF = ActivationFunctionType
NB2 = 4
NBV = 12 - NB2
ZS = 8
W1 = 131072.0
BASE = 640
WT = 4096 + 1024
SB = "sbuf"
F32, B16, F16, I32, U16 = "float32", "bfloat16", "float16", "int32", "uint16"
SCRATCH = {}
for _names, _w, _d in (
        ("TAB", WT, B16), ("OCC", WT, F32), ("ST", 1024 + WT, B16), ("EHT EFT", 1024, I32), ("ZFT", 1024, B16),
        ("IOT YD", 1024, F32), ("JM", 768, F32), ("QX", 144, F32), ("Q4", 128, F32), ("TMPF", 1024, F32), ("KCF JR M0 MI SCM SH SF WA WB YS Y1 Y2", 256, F32),
        ("PJ", 4, I32), ("PC", 8, F32), ("CI", 96, I32), ("CLA", 16, U16), ("CLB", 12, U16), ("DW C1", 48, I32), ("CJ2 WS", 192, F32),
        ("XV XS", 144, B16), ("X1", 144, F16), ("BO", 128, F16), ("BO16 BOB NID PID ZT1 ZT2", 128, B16), ("RO", 2048, B16), ("EX", 1024, B16),
        ("KC JRI", 256, B16), ("M0H", 768, F16), ("HH EE CO", 3072, B16), ("HF", 8, F32), ("SEH SEF", 192, U16), ("DL STN BN", 256, B16),
        ("EHO EFO", 256, U16), ("EI EM FI FM", 192, I32), ("ZX", 256 * NBV, B16), ("GB0 GB1", 1024, B16),
        ("IW", 64, I32), ("WF", 256, F32), ("KW NG INC", 16, B16), ("OH MSK SR", 256, F16), ("BL", 16, U16),
        ("FB VB", 784, F16), ("VW", 768, F16), ("VC", 8, F32), ("II", 288, I32), ("LU", 48, U16),
        ("ZL0 ZL1 ZL2 ZL3 RZ1 RZ2 RZ3", 256, B16), ("EHH0 EHH1 EHH2 EHH3", 256, F16), ("LW0 LW1 LW2 LW3", BASE + 1024, F32),
        ("FL0 FL1 FL2 FL3 WL0 WL1 WL2 WL3 RL1 RL2 RL3", 16, U16), ("FT0", 4096, B16), ("FT1 FT2 FT3", WT, B16)):
    for _n in _names.split():
        SCRATCH[_n] = (SB, [128, _w], _d)
for _n, _w in (("CH", NBV), ("CF", NBV), ("S1H", 4), ("S1F", 4), ("S2H", 4), ("S2F", 4)):
    SCRATCH[_n] = (SB, [128, _w, 256], B16)
for _n in ("KH", "KF", "D0", "D1", "SRP", "KRP", "SWP"):
    SCRATCH[_n] = ("psum", [128, 512], F32)
SCRATCH["ZTP"] = ("psum", [128, 1024], B16)
SEMAPHORES = ["cv", "cs", "cp", "cg"] + ["ld%d" % _i for _i in range(12)] + ["sn%d" % _i for _i in range(4)] + ["loc%d" % _i for _i in range(16)]
SEMAPHORES += ["rz%d" % _i for _i in range(4)] + ["rl%d" % _i for _i in range(4)] + ["out%d" % _i for _i in range(8)]
WIDX = {n: 16 * i for i, n in enumerate("SW NSW SD DTT WM GO NO WN GSD ND XW YW WN2 DT0 DT2".split())}


def make(g, T):
    eng = {"v": g.vector, "s": g.scalar, "p": g.tensor, "g": g, "y": g.sync}
    sem = {"v": "cv", "s": "cs", "p": "cp", "g": "cg"}
    cnt = {"v": 0, "s": 0, "p": 0, "g": 0}
    know = {e: {} for e in eng}
    acc, total = {}, {}

    def learn(e, tok):
        for k, v in tok[3].items():
            know[e][k] = max(v, know[e].get(k, 0))
        know[e][tok[0]] = max(tok[1], know[e].get(tok[0], 0))

    def psum(b):
        return b in SCRATCH and SCRATCH[b][0] == "psum"

    def needs(owner, reads, writes):
        out = []
        for mode, lst in (("r", reads), ("w", writes)):
            for (b, lo, hi) in lst:
                ps = psum(b)
                for (l2, h2, m2, tok) in acc.get(b, []):
                    if not ps and (h2 <= lo or hi <= l2):
                        continue
                    if mode == "r" and m2 == "r" and not ps:
                        continue
                    if tok[2] == owner and not (mode == "r" and m2 == "w"):
                        continue
                    out.append(tok)
        return out

    def waits(e, toks):
        for tok in sorted(toks, key=lambda x: (-len(x[3]), -x[1])):
            if know[e].get(tok[0], 0) < tok[1]:
                top = max([x for x in toks if x[0] == tok[0]], key=lambda x: x[1])
                eng[e].wait_ge(T.sem[top[0]], top[1])
                learn(e, top)

    def note(tok, reads, writes):
        for (b, lo, hi) in writes:
            lst = acc.setdefault(b, [])
            if not psum(b):
                lst[:] = [x for x in lst if not (lo <= x[0] and x[1] <= hi)]
            else:
                lst[:] = [x for x in lst if not (x[3][2] == tok[2] and x[2] == "w" and lo <= x[0] and x[1] <= hi)]
            lst.append((lo, hi, "w", tok))
        for (b, lo, hi) in reads:
            lst = acc.setdefault(b, [])
            lst[:] = [x for x in lst if not (x[2] == "r" and x[3][0] == tok[0] and lo <= x[0] and x[1] <= hi)]
            lst.append((lo, hi, "r", tok))

    def op(e, reads, writes, fn):
        waits(e, needs(e, reads, writes))
        cnt[e] += 1
        fn(eng[e]).then_inc(T.sem[sem[e]], 1)
        total[sem[e]] = cnt[e]
        note((sem[e], cnt[e], e, dict(know[e])), reads, writes)

    def dma(e, s, reads, writes, fn):
        waits(e, needs("dma" + s, reads, writes))
        fn(eng[e]).then_inc(T.sem[s], 16)
        total[s] = total.get(s, 0) + 16
        note((s, total[s], "dma" + s, dict(know[e])), reads, writes)

    def send(s, n, reads, fn):
        waits("g", needs("rem" + s, reads, []))
        fn(g)
        total[s] = total.get(s, 0) + n
        note((s, total[s], "rem" + s, dict(know["g"])), reads, [])

    def land(s, n, b, lo, hi):
        total[s] = total.get(s, 0) + n
        acc.setdefault(b, []).append((lo, hi, "w", (s, total[s], "net" + s, {})))

    def finish():
        for s, v in total.items():
            if know["g"].get(s, 0) < v:
                g.wait_ge(T.sem[s], v)
    return op, dma, send, land, finish


def rank_program(g, core, T, topo):
    rank = T.rank_of(core)
    if rank is None:
        return
    op, dma, send, land, finish = make(g, T)
    cores = T.cores

    def put(dst_buf, lo, hi, src_buf, peer, rsem, lsem):
        dst = cores[peer]
        rid, pid, _se = topo.addr(dst)
        send(lsem, len(topo.engines(core, dst)), [(src_buf, lo, hi)],
             lambda e: e.remote_dma(T[dst_buf][:, lo:hi], T[src_buf][:, lo:hi], T.sem[rsem], T.sem[lsem], pid, rid, topo.mask(core, dst)))

    def asker(t):
        return (rank - 1 - t % 3) % 4

    def nin(t):
        return len(topo.engines(cores[(rank + 1 + t % 3) % 4], core))

    def A(x):
        return T[x[0]][:, x[1]:x[2]]

    def w(n, a=0, b=16):
        return ("WF", WIDX[n] + a, WIDX[n] + b)

    def ts(o, i, s1, o0, s2=None, o1=None, ia=None, more=()):
        rd = [i] + list(more)
        src = A(i) if ia is None else ia
        if o1 is None:
            op("v", rd, [o], lambda e: e.tensor_scalar(A(o), src, s1, None, o0))
        else:
            op("v", rd, [o], lambda e: e.tensor_scalar(A(o), src, s1, s2, o0, o1))

    def tt(o, a, b, f, ia=None, ib=None, more=(), oa=None):
        op("v", [a, b] + list(more), [o], lambda e: e.tensor_tensor(A(o) if oa is None else oa, A(a) if ia is None else ia, A(b) if ib is None else ib, f))

    def cp(o, i, ia=None, oa=None, more=(), e="v"):
        src, out = A(i) if ia is None else ia, A(o) if oa is None else oa
        if e == "v":
            op("v", [i] + list(more), [o], lambda e: e.tensor_copy(out, src))
        else:
            op("s", [i] + list(more), [o], lambda e: e.activation(out, src, AF.Copy))

    def gather(o, win, lst, e="v", bias=None):
        if bias is None:
            cp(o, win, ia=A(win).indirect(A(lst)), more=[lst], e=e)
        else:
            op("s", [win, lst], [o], lambda e: e.activation(A(o), A(win).indirect(A(lst)), AF.Identity, bias=bias))

    def scatter(win, lst, i, more=()):
        cp(win, i, oa=A(win).indirect(A(lst)), more=[lst, win] + list(more))

    def scan(o, d0, d1, init, o0, o1):
        op("v", [d0, d1], [o], lambda e: e.tensor_tensor_scan(A(o), A(d0), A(d1), init, o0, o1))

    def mm(o, l, r, start, stop, oa=None, la=None, ra=None):
        op("p", [l, r], [o], lambda e: e.matmul(A(o) if oa is None else oa, A(l) if la is None else la, A(r) if ra is None else ra, start, stop))

    def iota(o, pattern, base, cm=0):
        op("g", [], [o], lambda e: e.iota(A(o), pattern, base, cm, allow_small_or_imprecise_dtypes=True))

    def memset(o, v):
        op("v", [], [o], lambda e: e.memset(A(o), v))

    def load(n, dst, lo, hi, src, a, b):
        dma("y", "ld%d" % n, [], [(dst, lo, hi)], lambda e: e.dma_start(T[dst][:, lo:hi], T[src][:, a:b]))
    load(0, "EHT", 192, 448, "eh", 0, 256)
    load(1, "ZFT", 192, 448, "zf", 0, 256)
    load(2, "TAB", 0, 2048, "tab", 0, 2048)
    load(3, "TAB", 2048, 4096, "tab", 2048, 4096)
    load(4, "EFT", 192, 448, "ef", 0, 256)
    for k, (dst, src) in enumerate((("EHT", "eh"), ("ZFT", "zf"), ("EFT", "ef"))):
        load(5 + 2 * k, dst, 0, 192, src, 832, 1024)
        load(6 + 2 * k, dst, 448, 1024, src, 256, 832)
    for t in range(4):
        land("sn%d" % t, nin(t) * (2 if t == 0 else 1), "FT%d" % t, 0, 4096)
    for t in range(1, 4):
        land("rz%d" % t, nin(t), "RZ%d" % t, 0, 256)
        land("rl%d" % t, nin(t), "RL%d" % t, 0, 16)

    pc = ("PC", 0, 4)
    iota(("PJ", 0, 1), [[0, 1]], 0, 1)
    iota(("CI", 0, 16), [[-16, 16]], 255)
    iota(("CI", 32, 44), [[-16, 12]], 191)
    iota(("QX", 0, 144), [[1, 144]], -15)
    iota(("Q4", 0, 128), [[16, 8], [0, 16]], 0)
    iota(("KCF", 0, 256), [[0, 16], [-8192, 16]], 122880)
    ts(("PJ", 2, 3), ("PJ", 0, 1), 15, OP.bitwise_and)
    ts(("PJ", 3, 4), ("PJ", 0, 1), 4, OP.arith_shift_right)
    cp(("PC", 0, 1), ("PJ", 2, 3))
    cp(("PC", 1, 2), ("PJ", 0, 1))
    ts(("PC", 2, 3), ("PJ", 3, 4), 16.0, OP.mult)
    ts(("PC", 3, 4), ("PJ", 2, 3), -1.0, OP.mult, 15.0, OP.add)
    PI_, PP, PG, P15 = T.PC[:, 0:1], T.PC[:, 1:2], T.PC[:, 2:3], T.PC[:, 3:4]
    ts(("CLA", 0, 16), ("CI", 0, 16), PI_, OP.subtract, more=[pc])
    ts(("CLB", 0, 12), ("CI", 32, 44), PI_, OP.subtract, more=[pc])
    memset(("HF", 0, 1), 0.5)
    qx = ("QX", 15, 143)
    ts(("NID", 0, 128), qx, PP, OP.is_equal, -1.0, OP.mult, more=[pc])
    ts(("PID", 0, 128), qx, PP, OP.is_equal, more=[pc])
    for n, f in (("XV", W1), ("XS", W1 / 2)):
        ts((n, 0, 144), ("QX", 0, 144), PG, OP.is_equal, f, OP.mult, more=[pc])
    ts(("BO16", 0, 128), ("Q4", 0, 128), PG, OP.is_equal, 0.0625, OP.mult, more=[pc])
    cp(("KC", 0, 16 * NBV), ("KCF", 0, 16 * NBV))
    ts(("KC", 16 * NBV, 256), ("KCF", 16 * NBV, 256), 8 * W1, OP.add)
    gather(("ZL0", 0, 256), ("ZFT", 192, 448), ("CLA", 0, 16), e="s")
    gather(("EHO", 0, 256), ("EHT", 192, 448), ("CLA", 0, 16))
    iota(("TMPF", 0, 1024), [[1, 64], [0, 16]], 0)
    ts(("EX", 0, 1024), ("TMPF", 0, 1024), PP, OP.is_equal, more=[pc])
    iota(("LW0", BASE, BASE + 256), [[-1, 256]], 447)
    iota(("JM", 0, 768), [[0, 48], [1, 16]], 0)
    iota(("JR", 0, 256), [[1, 256]], 0)
    for h in range(2):
        put("FT0", 2048 * h, 2048 * h + 2048, "TAB", asker(0), "sn0", "loc0")
    put("FT1", 0, 4096, "TAB", asker(1), "sn1", "loc1")
    put("RZ1", 0, 256, "ZL0", asker(1), "rz1", "loc4")
    iota(("CI", 48, 96), [[16, 48]], 65)
    iota(("OCC", 0, WT), [[1, WT]], 1024)
    iota(("IOT", 0, 1024), [[1, 1024]], 0)
    iota(("CJ2", 0, 192), [[-2, 192]], 382)
    for t in range(1, 4):
        iota(("LW%d" % t, BASE + 192, BASE + 256), [[-1, 64]], 255 - 64 * t)

    def constants_1():
        for (o, i, f) in ((("M0", 0, 256), ("JM", 0, 256), OP.not_equal), (("MI", 0, 256), ("JM", 0, 256), OP.is_equal)):
            ts(o, i, PI_, f, more=[pc])
        ts(("SCM", 0, 256), ("JM", 0, 256), 0.5, OP.is_gt)
        ts(("BOB", 0, 128), ("Q4", 0, 128), PG, OP.is_equal, more=[pc])
        for c in range(16):
            ts(("RO", 128 * c, 128 * c + 128), ("BOB", 0, 128), T.MI[:, c:c + 1], OP.mult, more=[("MI", 0, 256)])
        ts(("JRI", 0, 256), ("JR", 0, 256), PI_, OP.subtract, more=[pc])
        ts(("BO", 0, 128), ("Q4", 0, 128), PG, OP.is_equal, more=[pc])
        ts(("X1", 0, 144), ("QX", 0, 144), PG, OP.is_equal, more=[pc])
        ts(("EHH0", 0, 256), ("EHO", 0, 256), -2048.0, OP.add)

    def constants_s():
        for m in range(16):
            lo, n, a = (256 * m, 256, 0) if m < 8 else (2048 + 128 * (m - 8), 128, 128)
            op("s", [("JRI", a, 256)], [("HH", lo, lo + n)], lambda e: e.activation(T.HH[:, lo:lo + n], T.JRI[:, a:a + n], AF.Sign, bias=16.0 * m + 0.5, scale=-1.0))

    def constants_2():
        memset(("EE", 0, 3072), 1.0)
        memset(("ST", 0, 1024), 0.0)
        memset(("DL", 0, 256), 0.0)
        ts(("DW", 0, 48), ("CI", 48, 96), PI_, OP.add, more=[pc])
        ts(("C1", 0, 48), ("DW", 0, 48), float(BASE + 191), OP.add)
        ts(w("DT0"), ("DW", 0, 16), float(4096 - 65), OP.add)
        ts(("FL0", 0, 16), ("CLA", 0, 16), 192.0, OP.add)
        for (o, tab) in (("SEH", "EHT"), ("SEF", "EFT")):
            gather((o, 0, 192), (tab, 0, 192), ("CLB", 0, 12))
        for t in range(1, 4):
            x, l = 64 * (t - 1), ("CLB", 4 * t - 4, 4 * t)
            ts(("EHH%d" % t, 192, 256), ("SEH", x, x + 64), -2048.0, OP.add)
            gather(("ZL%d" % t, 192, 256), ("ZFT", 0, 192), l, e="s")
            cp(("FL%d" % t, 12, 16), l)
        ts(("M0H", 0, 768), ("JM", 0, 768), PI_, OP.not_equal, more=[pc])

    gbn = [0]

    def zt(t, j0, j1, dst):
        n, zl = j1 - j0, "ZL%d" % t
        op("p", [(zl, j0, j1), ("PID", 0, 128)], [("ZTP", 0, 128)], lambda e: e.transpose(T.ZTP[0:n, 0:128], T[zl][:, j0:j1], T.PID[:, :]))
        cp((dst, 0, 128), ("ZTP", 0, 128), ia=T.ZTP[0:n, 0:128], oa=T[dst][0:n, :], e="s")

    def s_gather(win, lst, c0, c1):
        gb = "GB%d" % (gbn[0] % 2)
        gbn[0] += 1
        gather((gb, 0, 16 * (c1 - c0)), (win, 0, 4096), (lst, c0, c1), e="s")
        return gb

    def s_diff(gb, ztb, nl):
        for h in range(nl // 32):
            x = 512 * h
            mm(("D%d" % h, 0, 512), (ztb, 0, 128), ("EX", x, x + 512), True, False, la=T[ztb][0:nl, :], ra=T.EX[0:nl, x:x + 512])
        for h in range(nl // 32):
            x = 512 * h
            mm(("D%d" % h, 0, 512), ("NID", 0, 128), (gb, x, x + 512), False, True)

    def s_sign(dst, nl):
        for m in range(nl // 16):
            d, x = "D%d" % (m // 2), 256 * (m % 2)
            op("s", [(d, x, x + 256), ("HF", 0, 1)], [(dst, 256 * m, 256 * m + 256)], lambda e: e.activation(T[dst][:, m, :], T[d][:, x:x + 256], AF.Sign, bias=T.HF[:, 0:1]))

    def sums(key, src, b0, b1, m0, xw, last):
        for c in range(16):
            mm((key, 16 * (m0 + b0), 16 * (m0 + b1)), (xw, 0, 144), (src, 256 * b0, 256 * b1), False, last and c == 15,
               la=T[xw][:, 15 - c:143 - c], ra=T[src][:, b0:b1, 16 * c:16 * c + 16])

    def key_open(key):
        mm((key, 0, 256), ("BO16", 0, 128), ("KC", 0, 256), True, False)

    def v_block(dst, win, lst, b):
        l, x = (lst, 16 * b, 16 * b + 16), (256 * b, 256 * b + 256)
        tt((dst, x[0], x[1]), (win, 0, 4096), ("ZX", x[0], x[1]), OP.is_le, ia=T[win][:, 0:4096].indirect(A(l)), more=[l], oa=T[dst][:, b, :])

    def spread(src, dst, start=True):
        for c in range(16):
            mm((dst, 0, 256), ("RO", 128 * c, 128 * c + 128), (src, 0, 16), start, start or c == 15, oa=T[dst][:, c:256:16])

    nb2j = 192 - 16 * NB2

    def fresh(t):
        return ("EHO", "EFO", 192) if t == 0 else ("SEH", "SEF", 64 * (t - 1))

    def fresh_home(t):
        lst, _f, c0 = fresh(t)
        zt(t, 192, 256, "ZT1")
        gb = s_gather("TAB", lst, c0, c0 + 64)
        s_diff(gb, "ZT1", 64)
        s_sign("S1H", 64)
        key_open("KH")
        sums("KH", "S1H", 0, 4, 12, "XS", False)

    def fresh_foreign(t):
        _h, lst, c0 = fresh(t)
        gb = s_gather("FT%d" % t, lst, c0, c0 + 64)
        key_open("KF")
        s_diff(gb, "ZT1", 64)
        s_sign("S1F", 64)
        sums("KF", "S1F", 0, 4, 12, "XS", False)

    def expand(t):
        for kk in range(16):
            cp(("ZX", 0, 256 * NBV), ("ZL%d" % t, 0, 16 * NBV), oa=T.ZX[:, kk:256 * NBV:16], e="s" if kk < ZS else "v")

    def step_main(t):
        ft, half = "FT%d" % t, (NBV + 1) // 2
        if t:
            expand(t)
        for b in range(NBV):
            v_block("CH", "TAB", "EHO", b)
        zt(t, nb2j, 192, "ZT2")
        ga = s_gather("TAB", "EHO", nb2j, 192)
        if t:
            gb = s_gather(ft, "EFO", nb2j, 192)
        s_diff(ga, "ZT2", 16 * NB2)
        s_sign("S2H", 16 * NB2)
        sums("KH", "CH", 0, half, 0, "XV", False)
        sums("KH", "S2H", 0, NB2, NBV, "XS", False)
        sums("KH", "CH", half, NBV, 0, "XV", True)
        if t == 0:
            gather(("EFO", 0, 256), ("EFT", 192, 448), ("CLA", 0, 16))
            constants_1()
            constants_s()
            claim_slots_1(t)
            fresh_foreign(0)
            gb = s_gather(ft, "EFO", nb2j, 192)
        s_diff(gb, "ZT2", 16 * NB2)
        s_sign("S2F", 16 * NB2)
        for b in range(half):
            v_block("CF", ft, "EFO", b)
        if t:
            claim_slots_1(t)
        sums("KF", "CF", 0, half, 0, "XV", False)
        for b in range(half, NBV):
            v_block("CF", ft, "EFO", b)
        if t == 0:
            constants_2()
        claim_slots_2(t)
        sums("KF", "S2F", 0, NB2, NBV, "XS", False)
        sums("KF", "CF", half, NBV, 0, "XV", True)

    def claim_slots_1(t):
        scan(("SH", 0, 256), ("SCM", 0, 256), ("KH", 0, 256), 0.0, OP.mult, OP.max)
        cp(("IW", 0, 16), ("SH", 0, 256), ia=T.SH[:, 15:256:16])
        ts(("IW", 16, 32), ("IW", 0, 16), 13, OP.arith_shift_right, 15, OP.bitwise_and)
        cp(("KW", 0, 16), ("IW", 16, 32))
        spread("KW", "KRP")

    def claim_slots_2(t):
        ts(("OH", 0, 256), ("KRP", 0, 256), P15, OP.is_equal, more=[pc])
        tt(("MSK", 0, 256), ("OH", 0, 256), ("EHH%d" % t, 0, 256), OP.mult)
        mm(("SRP", 0, 256), ("BO", 0, 128), ("MSK", 0, 256), True, False)
        for i in range(16):
            mm(("SWP", 0, 16), ("X1", 15 - i, 143 - i), ("MSK", 0, 256), i == 0, i == 15, ra=T.MSK[:, i:256:16])
        op("s", [("SWP", 0, 16)], [w("NSW")], lambda e: e.activation(A(w("NSW")), T.SWP[:, 0:16], AF.Copy, scale=-1.0))
        ts(w("DTT"), w("DT0"), float(256 * t), OP.add)
        ts(w("DT2"), w("DT0"), float(256 * t - 2048), OP.add)

    def step_claims(t):
        wl = ("WL%d" % t, 0, 16)
        cp(w("SW"), ("SWP", 0, 16))
        tt(w("SD"), w("SW"), w("DT2"), OP.subtract)
        scan(("SF", 0, 256), ("SCM", 0, 256), ("KF", 0, 256), 0.0, OP.mult, OP.max)
        tt(w("WM"), ("SH", 0, 256), ("SF", 0, 256), OP.max, ia=T.SH[:, 15:256:16], ib=T.SF[:, 15:256:16])
        ts(("NG", 0, 16), w("WM"), 9 * W1, OP.is_ge, 8192.0, OP.mult)
        spread("NG", "SRP", False)
        ts(w("GO"), w("WM"), 9 * W1, OP.is_lt)
        ts(w("NO"), w("WM"), 9 * W1, OP.is_ge)
        cp(("IW", 32, 48), w("WM"))
        tt(w("GSD"), w("GO"), w("SD"), OP.mult)
        ts(("IW", 48, 64), ("IW", 32, 48), 17, OP.arith_shift_right)
        cp(("SR", 0, 256), ("SRP", 0, 256))
        for m in (0, 15, 1, 14, 2, 13, 3, 12, 11, 10, 9, 8, 4, 5, 6, 7):
            end = 256 * m + 256 if m < 8 else 2048 + 128 * (m - 7)
            o, i = ("EE", end - 256 + 16 * m, end), (16 * m, 256)
            if m < 4:
                op("s", [("SRP", i[0], 256), w("NSW")], [o], lambda e: e.activation(A(o), T.SRP[:, i[0]:256], AF.Abs, bias=A(w("NSW", m, m + 1))))
            else:
                ts(o, ("SR", i[0], 256), A(w("SW", m, m + 1)), OP.not_equal, more=[w("SW")])
        tt(w("WN"), ("IW", 48, 64), w("NO"), OP.mult)
        for (lo, hi, st, a) in ((2048, 3072, 128, 8), (0, 2048, 256, 0)):
            scan(("CO", lo, hi), ("EE", lo, hi), ("HH", lo, hi), 1.0, OP.min, OP.max)
        for (lo, hi, st, a) in ((2048, 3072, 128, 8), (0, 2048, 256, 0)):
            ts(w("ND", a, a + 8), ("CO", lo, hi), 0.25, OP.is_gt, ia=T.CO[:, lo + st - 1:hi:st])
        tt(w("XW"), w("ND"), w("GSD"), OP.mult)
        tt(w("WN2"), w("ND"), w("GO"), OP.mult)
        tt(w("YW"), w("XW"), w("DTT"), OP.add)
        ts(w("WN2"), w("WN2"), 128.0, OP.mult)
        cp(wl, w("YW"))
        tt(("INC", 0, 16), w("WN"), w("WN2"), OP.add)
        spread("INC", "KRP")
        scatter(("TAB", 0, WT), wl, ("ZL%d" % t, 0, 256))

    def out_table(h):
        dma("y", "out%d" % h, [("TAB", 2048 * h, 2048 * h + 2048)], [("yt", 2048 * h, 2048 * h + 2048)],
            lambda e: e.dma_start(T.yt[:, 2048 * h:2048 * h + 2048], T.TAB[:, 2048 * h:2048 * h + 2048]))

    def step_state(t):
        wl, fl = ("WL%d" % t, 0, 16), ("FL%d" % t, 0, 16)
        st, st0 = ("ST", 0, 1024 + WT), ("ST", 0, 1024)
        if t:
            tt(("WA", 0, 256), ("OCC", 0, WT), ("MI", 0, 256), OP.mult, ia=T.OCC[:, :].indirect(A(wl)), more=[wl])
        if t == 3:
            out_table(0)
            occ(t)
            dma("y", "out2", [("OCC", 0, 4096)], [("YS", 0, 256)], lambda e: e.dma_start(T.YS[:, :], T.OCC[0:128:16, 0:4096]))
            out_table(1)
        if t:
            scan(("WB", 0, 256), ("M0", 0, 256), ("WA", 0, 256), 0.0, OP.mult, OP.add)
            cp(("BL", 0, 16), ("WB", 0, 256), ia=T.WB[:, 15:256:16])
            gather(("BN", 0, 256), st, ("BL", 0, 16), e="s", bias=-127.0)
        tt(("STN", 0, 256), ("KRP", 0, 256), ("DL", 0, 256), OP.add)
        scatter(st0, fl, ("STN", 0, 256))
        if t:
            scatter(st, ("BL", 0, 16), ("BN", 0, 256))

    def occ(t):
        scatter(("OCC", 0, WT), ("WL%d" % t, 0, 16), ("LW%d" % t, BASE, BASE + 256), more=[("WA", 0, 256)])

    def step_select(t):
        U, lo = 256 * t, 256 - 64 * t
        new, n = lo + U, 16 * t
        lw, fl, zl = "LW%d" % t, ("FL%d" % t, 0, 12), ("ZL%d" % t, 0, 192)
        if t == 1:
            ts(("FB", 0, 1), ("DL", 0, 1), 0.0, OP.mult)
        ts(("FB", U + 1, U + 2), ("DL", 0, 1), 0.0, OP.mult, -1.0, OP.add)
        ts(("FB", 1, U + 1), ("ST", lo, lo + U), 128.0, OP.is_lt, -1.0, OP.mult)
        scan(("VB", 0, U + 1), ("FB", 1, U + 2), ("FB", 0, U + 1), 2000.0, OP.add, OP.add)
        scan(("VW", 0, U), ("M0H", 0, U), ("VB", 0, U), 0.0, OP.mult, OP.max)
        ts(("VC", 0, 1), ("VB", U, U + 1), float(2 * new - 1999), OP.add)

        def I(k):
            return ("II", 48 * k, 48 * k + n)
        ts(I(0), ("VW", 0, U), -1.0, OP.mult, 2000.0, OP.add, ia=T.VW[:, 15:U:16])
        ts((lw, BASE, BASE + 192), ("CJ2", 0, 192), T.VC[:, 0:1], OP.add, 0.5, OP.mult, more=[("VC", 0, 1)])
        ts(I(1), I(0), 1, OP.bitwise_and)
        ts(I(2), I(0), 1, OP.arith_shift_right)
        tt(I(3), I(1), ("DW", 0, n), OP.mult)
        tt(I(4), ("C1", 0, n), I(2), OP.subtract)
        tt(I(5), I(4), I(3), OP.subtract)
        cp(("LU", 0, n), I(5))
        scatter((lw, 0, BASE + 1024), ("LU", 0, n), ("IOT", lo, lo + U))
        scan(("WS", 0, 192), ("M0", 0, 192), (lw, BASE, BASE + 192), 0.0, OP.mult, OP.max)
        cp(fl, ("WS", 0, 192), ia=T.WS[:, 15:192:16])
        occ(t - 1)
        gather(("DL", 0, 192), ("ST", 0, 1024), fl, e="s")
        gather(zl, ("ZFT", 0, 1024), fl, e="s")
        for (tab, a, b, o) in (("EHT", "EI", "EM", "EHO"), ("EFT", "FI", "FM", "EFO")):
            tt((a, 0, 192), (tab, 0, 1024), ("DL", 0, 192), OP.add, ia=T[tab][:, :].indirect(A(fl)), more=[fl])
            ts((b, 0, 192), (a, 0, 192), 4095, OP.bitwise_and)
            cp((o, 0, 192), (b, 0, 192))
        ts(("EHH%d" % t, 0, 192), ("EM", 0, 192), -2048.0, OP.add)

    memset(("WA", 0, 256), 0.0)
    expand(0)
    fresh_home(0)
    for t in range(4):
        if t:
            step_select(t)
            if t < 3:
                put("RZ%d" % (t + 1), 0, 256, "ZL%d" % t, asker(t + 1), "rz%d" % (t + 1), "loc%d" % (4 + t))
        step_main(t)
        step_claims(t)
        u = t + 1
        if t < 3:
            dst = cores[asker(u)]
            rid, pid, _se = topo.addr(dst)
            send("loc%d" % (8 + t), len(topo.engines(core, dst)), [("WL%d" % t, 0, 16)],
                 lambda e: e.remote_dma(T["RL%d" % u][:, :], T["WL%d" % t][:, :], T.sem["rl%d" % u], T.sem["loc%d" % (8 + t)], pid, rid, topo.mask(core, dst)))
        if t < 2:
            put("FT%d" % (t + 2), 0, 4096, "TAB", asker(t + 2), "sn%d" % (t + 2), "loc%d" % (12 + t))
        if t == 0:
            iota(("ST", 1024, 1024 + WT), [[0, WT]], 0)
        step_state(t)
        if t < 3:
            fresh_home(u)
            scatter(("FT%d" % u, 0, WT), ("RL%d" % u, 0, 16), ("RZ%d" % u, 0, 256))
            fresh_foreign(u)
    ts(("GB0", 0, 1024), ("ST", 0, 1024), 128.0, OP.is_ge, -128.0, OP.mult)
    for h in range(2):
        d, x = ("D%d" % h, 0, 512), (512 * h, 512 * h + 512)
        mm(d, ("PID", 0, 128), ("ST", x[0], x[1]), True, False)
        mm(d, ("PID", 0, 128), ("GB0", x[0], x[1]), False, True)
        cp(("YD", x[0], x[1]), d, e="s")
    ys, y1, y2 = ("YS", 0, 256), ("Y1", 0, 256), ("Y2", 0, 256)
    ts(y1, ys, 192.0, OP.is_lt, 1024.0, OP.mult)
    ts(y2, ys, 1024.0, OP.is_lt)
    tt(y1, ys, y1, OP.add)
    ts(y1, y1, -191.0, OP.add)
    tt(y1, y1, y2, OP.mult)
    ts(y1, y1, -1.0, OP.add)
    dma("y", "out5", [y1], [("yo", 0, 4096)], lambda e: e.dma_start(T.yo[:, :], T.Y1[:, :]))
    dma("s", "out3", [("YD", 192, 1024)], [("yd", 0, 832)], lambda e: e.dma_start(T.yd[:, 0:832], T.YD[0:128:16, 192:1024]))
    dma("s", "out4", [("YD", 0, 192)], [("yd", 832, 1024)], lambda e: e.dma_start(T.yd[:, 832:1024], T.YD[0:128:16, 0:192]))
    finish()
